import numpy as np
import ml_dtypes


def mxq(x, axis, fmt="e4m3"):
    dtype, down = {"e4m3": (ml_dtypes.float8_e4m3fn, 7), "e5m2": (ml_dtypes.float8_e5m2, 14)}[fmt]
    v = np.moveaxis(np.asarray(x, np.float32).astype(ml_dtypes.bfloat16).astype(np.float64), axis, -1)
    blocks = v.reshape(v.shape[:-1] + (-1, 32))
    amax = np.abs(blocks).max(-1, keepdims=True)
    byte = np.maximum(np.where(amax > 0, np.frexp(amax)[1] - 1 + 127, 0) - down, 1)
    scale = np.exp2(byte - 127.0)
    codes = (blocks / scale).astype(np.float32).astype(dtype).astype(np.float64)
    return np.moveaxis((codes * scale).reshape(v.shape), -1, axis)


WIDE = False


def mx_kscale(k):
    if not WIDE:
        return np.ones(k)
    levels = np.array([10, -10, 5, -5, 0])
    if k % 512:
        return np.exp2(np.random.permutation(np.resize(levels, k // 32))).repeat(32)
    a = np.empty((k // 512, 16))
    for p in range(k // 512):
        a[p, :8] = np.random.permutation(np.resize(levels, 8))
        for g in range(8):
            far = levels[np.abs(levels - a[p, g]) >= 10]
            a[p, g + 8] = far[np.random.randint(len(far))]
    return np.exp2(a.ravel()).repeat(32)


def f64(x):
    return np.asarray(x).astype(np.float64)


def striped(idx):
    return np.tile(np.asarray(idx).reshape(-1, 16).T, (8, 1)).astype(np.uint16)


def unstriped(offs):
    return offs[:16].T.reshape(-1).astype(np.int64)


E2M1 = np.array([0.0, 0.5, 1.0, 1.5, 2.0, 3.0, 4.0, 6.0, -0.0, -0.5, -1.0, -1.5, -2.0, -3.0, -4.0, -6.0])


def pack_weight(w, fmt):
    k, n = w.shape
    w = f64(np.asarray(w, np.float32).astype(ml_dtypes.bfloat16)).reshape(k // 32, 32, n)
    amax = np.abs(w).max(1)
    if fmt == "e4m3":
        byte = np.frexp(amax)[1] - 1 + 127 - 7
    else:
        mant, ex = np.frexp(amax / 6.0)
        byte = np.where(mant > 0.5, ex, ex - 1) + 127
    byte = np.clip(np.where(amax > 0, byte, 1), 1, 254)
    scaled = (w * np.exp2(127.0 - byte)[:, None, :]).reshape(k, n).astype(np.float32)
    by_word = np.ascontiguousarray(scaled.reshape(k // 512, 128, 4, n).transpose(0, 1, 3, 2))
    if fmt == "e4m3":
        words = by_word.astype(ml_dtypes.float8_e4m3fn).view(np.uint8)
    else:
        c = by_word.astype(ml_dtypes.float4_e2m1fn).view(np.uint8) & 0xF
        words = (c[..., 0::2] | (c[..., 1::2] << 4)).reshape(k // 512, 128, 2 * n)
    return np.ascontiguousarray(words), np.ascontiguousarray(byte.astype(np.uint8).reshape(k // 512, 16, n))


def unpack_weight(words, scales, fmt):
    g, _, n = scales.shape
    words = np.ascontiguousarray(words).reshape(g, 128, n, -1)
    if fmt == "e4m3":
        vals = words.view(ml_dtypes.float8_e4m3fn).astype(np.float64)
    else:
        nib = np.empty((g, 128, n, 4), np.uint8)
        nib[..., 0::2] = words & 0xF
        nib[..., 1::2] = words >> 4
        vals = E2M1[nib]
    vals = vals * np.repeat(np.exp2(scales.astype(np.float64) - 127.0), 8, axis=1)[..., None]
    return vals.transpose(0, 1, 3, 2).reshape(g * 512, n)


def bf(x):
    return np.asarray(x, np.float32).astype(ml_dtypes.bfloat16)


def planes(Y):
    r, m = Y.shape
    b = f64(bf(Y)).reshape(r // 32, 32, m)
    amax = np.abs(b).max(1)
    byte = np.clip(np.where(amax > 0, np.frexp(amax)[1] - 1 + 127 - 7, 1), 1, 254)
    codes = (b * np.exp2(127.0 - byte)[:, None, :]).reshape(r, m).astype(np.float32).astype(ml_dtypes.float8_e4m3fn).view(np.uint8)
    words = codes.reshape(r // 512, 128, 4, m).transpose(0, 1, 3, 2)
    return np.ascontiguousarray(words), np.ascontiguousarray(byte.astype(np.uint8).reshape(r // 512, 16, m))


D, E, T, I, Q = 512, 512, 2048, 512, 256


def setup_inputs():
    n = np.random.standard_normal
    idx = np.random.permutation(T)[:I]
    fd = mx_kscale(D)
    fi = mx_kscale(I)
    ti = np.ones(T)
    ti[idx] = fi
    keysp = pack_weight(n((D, T)) / fd[:, None], "e2m1")
    return {
        "query": (n((D, Q)) * 0.35 / np.sqrt(D) * fd[:, None]).astype(np.float32),
        "dquery": (n((D, Q)) * 0.6 / np.sqrt(D) * fd[:, None]).astype(np.float32),
        "query2": (n((D, Q)) * 0.35 / np.sqrt(D) * fd[:, None]).astype(np.float32),
        "dquery2": (n((D, Q)) * 0.6 / np.sqrt(D) * fd[:, None]).astype(np.float32),
        "keys_words": keysp[0],
        "keys_scales": keysp[1],
        "os": (np.random.uniform(4.0, 16.0, (1, I)) * fi).astype(np.float32),
        "vals": (n((E, T)) / ti).astype(np.float32),
        "offs": striped(idx),
    }


def reference(query, dquery, query2, dquery2, keys_words, keys_scales, os, vals, offs):
    idx = unstriped(offs)
    keysu = unpack_weight(keys_words, keys_scales, "e2m1")
    queryq = mxq(f64(query), 0, "e4m3")
    keysidxg = keysu[:, idx]
    a = queryq.T @ keysidxg
    dqueryq = mxq(f64(dquery), 0, "e4m3")
    ta = dqueryq.T @ keysidxg
    query2q = mxq(f64(query2), 0, "e4m3")
    b = query2q.T @ keysidxg
    dquery2q = mxq(f64(dquery2), 0, "e4m3")
    tb = dquery2q.T @ keysidxg
    s = a * (b + 1.0)
    p = np.exp(s - np.max(s, axis=1, keepdims=True))
    ts = ta * (b + 1.0) + tb * a
    tp = ts * p
    tw = (tp - np.sum(tp, axis=1, keepdims=True) * p / np.sum(p, axis=1, keepdims=True)) / np.sum(p, axis=1, keepdims=True)
    wo1 = tw * f64(os)
    wt1 = wo1.T
    vt1 = f64(vals)[:, idx].T
    vt1q = mxq(vt1, 0, "e4m3")
    wt1q = mxq(wt1, 0, "e4m3")
    o = vt1q.T @ wt1q
    words, scales = planes(o)
    return o, words, scales

@@ -1,0 +1,267 @@
+from contextlib import ExitStack
+
+import concourse.mybir as mybir
+from concourse.masks import make_identity
+
+D, E, T, I, Q = 512, 512, 2048, 512, 256
+FLOPS = 4 * 2 * Q * D * I + 2 * E * I * Q
+
+F32 = mybir.dt.float32
+BF16 = mybir.dt.bfloat16
+I32 = mybir.dt.int32
+U32 = mybir.dt.uint32
+U16 = mybir.dt.uint16
+U8 = mybir.dt.uint8
+FP8X4 = mybir.dt.float8_e4m3fn_x4
+FP4X4 = mybir.dt.float4_e2m1fn_x4
+ALU = mybir.AluOpType
+ACT = mybir.ActivationFunctionType
+AX = mybir.AxisListType
+
+P = 128
+PACK = 4
+QT = Q // P
+
+
+def dealt(bank):
+    return bank[:].rearrange("p (s j) -> p j s", j=PACK)
+
+
+def by_place(tile):
+    return tile[:].rearrange("p (j s) -> p j s", j=PACK)
+
+
+def tile_attend_ttproductscore_pl_kernel(tc, query, dquery, query2, dquery2, keys_words, keys_scales, slot_factor, vals, offs, out_0, out_1, out_2):
+    nc = tc.nc
+    with ExitStack() as ctx:
+        sb = ctx.enter_context(tc.tile_pool(name="sb", bufs=1))
+        ps = ctx.enter_context(tc.psum_pool(name="ps", bufs=1))
+
+        offsets = sb.tile([P, I // 16], U16, name="offsets")
+        kw = sb.tile([P, T], U16, name="kw", align_bytes=64)
+        ks = sb.tile([P, T], U8, name="ks", align_bytes=64)
+        nc.gpsimd.memset(ks[:].bitcast(I32), 0)
+        ident = sb.tile([P, P], F32, name="ident")
+        make_identity(nc, ident[:])
+
+        nc.sync.dma_start(offsets[:], offs)
+        for g in range(4):
+            nc.scalar.dma_start(out=ks[32 * g : 32 * g + 4, :].bitcast(I32), in_=keys_scales[0, 4 * g : 4 * g + 4, :].bitcast(I32))
+        nc.sync.dma_start(out=kw[:].bitcast(I32), in_=keys_words[0].bitcast(I32))
+        os4 = sb.tile([P, 1, PACK], F32, name="os4")
+        nc.scalar.dma_start(out=os4[:, 0, :], in_=slot_factor.rearrange("o (s j) -> (o s) j", j=PACK))
+        warm2 = sb.tile([P, 1], F32, name="warm2")
+        nc.scalar.activation(out=warm2[:], in_=ident[:, 0:1], func=ACT.Exp)
+        names = ("a", "b", "ta", "tb")
+        raw = {}
+        for n, src in zip(names, (query, query2, dquery, dquery2)):
+            raw[n] = sb.tile([P, PACK, Q], F32, name="raw_" + n)
+            nc.sync.dma_start(out=raw[n][:], in_=src.rearrange("(p j) w -> p j w", j=PACK))
+        vwin = []
+        for r in range(PACK):
+            w = sb.tile([P, T], F32, name="vwin%d" % r)
+            nc.sync.dma_start(out=w[:], in_=vals.rearrange("(p r) t -> r p t", r=PACK)[r])
+            vwin.append(w)
+
+        kwg = sb.tile([P, I], U16, name="kwg", align_bytes=64)
+        ksg = sb.tile([P, I], U8, name="ksg", align_bytes=64)
+        nc.vector.tensor_copy(ksg[:], ks[:].indirect(offsets[:]))
+        nc.vector.tensor_copy(kwg[:], kw[:].indirect(offsets[:]))
+
+        qb, qc, qs, bank = {}, {}, {}, {}
+
+        def weave(n, h0, h1, on_vector):
+            width = (h1 - h0) * P
+            g = sb.tile([P, width, PACK], BF16, name="qb_%s%d" % (n, h0), align_bytes=64)
+            dst = g[:].rearrange("p (c i) t -> p c t i", i=4)
+            src = raw[n][:, :, h0 * P : h1 * P].rearrange("p t (c i) -> p c t i", i=4)
+            if on_vector:
+                nc.vector.tensor_copy(out=dst, in_=src)
+            else:
+                nc.scalar.copy(out=dst, in_=src)
+            qb[n, h0] = g
+
+        def quant_q(n, h0, h1):
+            width = (h1 - h0) * P
+            cd = sb.tile([P, width], U32, name="qc_%s%d" % (n, h0), align_bytes=64)
+            sc = sb.tile([P, width], U8, name="qs_%s%d" % (n, h0), align_bytes=64)
+            nc.vector.quantize_mx(out=cd[:].bitcast(FP8X4), scales=sc[:], in_=qb[n, h0][:].rearrange("p w j -> p (w j)"))
+            for h in range(h0, h1):
+                cols = slice((h - h0) * P, (h - h0 + 1) * P)
+                qc[n, h] = cd[:, cols]
+                qs[n, h] = sc[:, cols]
+
+        def score(n, h):
+            bank[n, h] = ps.tile([P, I], F32, name="s_%s%d" % (n, h), tag="bank_%s%d" % (n, h))
+            nc.tensor.matmul_mx(out=bank[n, h][:], lhsT=qc[n, h].bitcast(FP8X4), lhsT_scale=qs[n, h],
+                                rhs=kwg[:].bitcast(FP4X4), rhs_scale=ksg[:], start=True, stop=True)
+
+        def f32tile(name, cols=I):
+            return sb.tile([P, cols], F32, name=name)
+
+        a_sb = [f32tile("a_sb%d" % h) for h in range(QT)]
+        b1 = [f32tile("b1_%d" % h) for h in range(QT)]
+        s = [f32tile("s%d" % h) for h in range(QT)]
+        p = [f32tile("p%d" % h) for h in range(QT)]
+        u = [f32tile("u%d" % h) for h in range(QT)]
+        v = [f32tile("v%d" % h) for h in range(QT)]
+        ts = [f32tile("ts%d" % h) for h in range(QT)]
+        tp = [f32tile("tp%d" % h) for h in range(QT)]
+        z = [f32tile("z%d" % h) for h in range(QT)]
+        negmax = [f32tile("negmax%d" % h, 1) for h in range(QT)]
+        zsum = [f32tile("zsum%d" % h, 1) for h in range(QT)]
+        rz = [f32tile("rz%d" % h, 1) for h in range(QT)]
+        nrz = [f32tile("nrz%d" % h, 1) for h in range(QT)]
+        c = [f32tile("c%d" % h, 1) for h in range(QT)]
+        k = [f32tile("k%d" % h, 1) for h in range(QT)]
+        wT, wb, wc, ws, vg, vb, vc, vs = {}, {}, {}, {}, {}, {}, {}, {}
+
+        def copy_a(h):
+            nc.scalar.copy(out=by_place(a_sb[h]), in_=dealt(bank["a", h]))
+
+        def copy_b(h):
+            nc.scalar.activation(out=by_place(b1[h]), in_=dealt(bank["b", h]), func=ACT.Copy, bias=1.0)
+
+        def make_s(h):
+            nc.vector.scalar_tensor_tensor(out=by_place(s[h]), in0=dealt(bank["b", h]), scalar=1.0, in1=by_place(a_sb[h]), op0=ALU.add, op1=ALU.mult)
+
+        def make_max(h):
+            nc.vector.tensor_reduce(out=negmax[h][:], in_=s[h][:], axis=AX.X, op=ALU.max, negate=True)
+
+        def make_p(h):
+            nc.scalar.activation(out=p[h][:], in_=s[h][:], func=ACT.Exp, bias=negmax[h][:], accum_out=zsum[h][:])
+
+        def make_u(h):
+            nc.vector.tensor_tensor(out=by_place(u[h]), in0=dealt(bank["ta", h]), in1=by_place(b1[h]), op=ALU.mult)
+
+        def make_v(h):
+            nc.vector.tensor_tensor(out=by_place(v[h]), in0=dealt(bank["tb", h]), in1=by_place(a_sb[h]), op=ALU.mult)
+
+        def make_rz(h):
+            nc.vector.reciprocal(out=rz[h][:], in_=zsum[h][:])
+            nc.scalar.activation(out=nrz[h][:], in_=rz[h][:], func=ACT.Copy, scale=-1.0)
+
+        def make_ts(h, eng):
+            eng.tensor_tensor(out=ts[h][:], in0=u[h][:], in1=v[h][:], op=ALU.add)
+
+        def make_tp(h):
+            nc.vector.scalar_tensor_tensor(out=tp[h][:], in0=ts[h][:], scalar=rz[h][:], in1=p[h][:], op0=ALU.mult, op1=ALU.mult, accum_out=c[h][:])
+            nc.scalar.activation(out=k[h][:], in_=c[h][:], func=ACT.Copy, scale=nrz[h][:])
+            nc.scalar.activation(out=z[h][:], in_=p[h][:], func=ACT.Copy, scale=k[h][:])
+            t = ps.tile([P, PACK, P], F32, name="wT%d" % h, tag="bank_ta%d" % h)
+            for j in range(PACK):
+                cols = slice(j * P, (j + 1) * P)
+                nc.tensor.matmul(out=t[:, j, :], lhsT=tp[h][:, cols], rhs=ident[:], start=True, stop=False, is_transpose=True)
+                nc.tensor.matmul(out=t[:, j, :], lhsT=z[h][:, cols], rhs=ident[:], start=False, stop=True, is_transpose=True)
+            wT[h] = t
+
+        def gather_v(r, on_vector):
+            g = sb.tile([P, I], BF16, name="vg%d" % r, align_bytes=64)
+            if on_vector:
+                nc.vector.tensor_copy(g[:], vwin[r][:].indirect(offsets[:]))
+            else:
+                w16 = sb.tile([P, T], BF16, name="vwin16_%d" % r, align_bytes=64)
+                nc.scalar.activation(out=w16[:], in_=vwin[r][:], func=ACT.Copy)
+                nc.scalar.activation(out=g[:], in_=w16[:].indirect(offsets[:]), func=ACT.Copy)
+            words = g[:].bitcast(F32)
+            t = ps.tile([P, 2, P], F32, name="vT%d" % r, tag="bank_a%d" % (r % 2))
+            for half in range(2):
+                nc.tensor.transpose(t[:, half, :], words[:, half : I // 2 : 2], ident[:])
+            vb[r] = sb.tile([P, P * PACK], BF16, name="vb%d" % r, align_bytes=64)
+            nc.scalar.copy(out=vb[r][:].bitcast(F32).rearrange("p (e u) -> p e u", u=2), in_=t[:].rearrange("p u e -> p e u"))
+
+        def quant_v(r):
+            vc[r] = sb.tile([P, P], U32, name="vc%d" % r, align_bytes=64)
+            vs[r] = sb.tile([P, P], U8, name="vs%d" % r, align_bytes=64)
+            nc.vector.quantize_mx(out=vc[r][:].bitcast(FP8X4), scales=vs[r][:], in_=vb[r][:])
+
+        def weights(h):
+            wb[h] = sb.tile([P, P, PACK], BF16, name="wb%d" % h, align_bytes=64)
+            nc.vector.tensor_tensor(out=wb[h][:], in0=wT[h][:].rearrange("p j q -> p q j"), in1=os4[:].to_broadcast([P, P, PACK]), op=ALU.mult)
+
+        def quant_w(h):
+            wc[h] = sb.tile([P, P], U32, name="wc%d" % h, align_bytes=64)
+            ws[h] = sb.tile([P, P], U8, name="ws%d" % h, align_bytes=64)
+            nc.vector.quantize_mx(out=wc[h][:].bitcast(FP8X4), scales=ws[h][:], in_=wb[h][:].rearrange("p q j -> p (q j)"))
+
+        ob = {}
+
+        def product(r, h):
+            if h not in ob:
+                ob[h] = ps.tile([P, PACK, P], F32, name="o%d" % h, tag="bank_b%d" % h)
+            nc.tensor.matmul_mx(out=ob[h][:, r, :], lhsT=vc[r][:].bitcast(FP8X4), lhsT_scale=vs[r][:],
+                                rhs=wc[h][:].bitcast(FP8X4), rhs_scale=ws[h][:], start=True, stop=True)
+
+        weave("a", 0, 1, False)
+        weave("a", 1, 2, False)
+        quant_q("a", 0, 1)
+        weave("b", 0, 1, True)
+        weave("b", 1, 2, False)
+        quant_q("a", 1, 2)
+        quant_q("b", 0, 1)
+        score("a", 0)
+        score("b", 0)
+        quant_q("b", 1, 2)
+        score("a", 1)
+        score("b", 1)
+        copy_a(0)
+        weave("ta", 0, 2, True)
+        copy_a(1)
+        make_s(0)
+        quant_q("ta", 0, 2)
+        weave("tb", 0, 2, False)
+        make_s(1)
+        make_max(0)
+        score("ta", 0)
+        score("ta", 1)
+        quant_q("tb", 0, 2)
+        score("tb", 0)
+        score("tb", 1)
+        make_max(1)
+        copy_b(0)
+        make_p(0)
+        copy_b(1)
+        make_p(1)
+        make_v(0)
+        make_u(0)
+        make_rz(0)
+        make_v(1)
+        make_ts(0, nc.vector)
+        make_u(1)
+        make_tp(0)
+        make_rz(1)
+        make_ts(1, nc.vector)
+        gather_v(0, False)
+        gather_v(1, True)
+        weights(0)
+        gather_v(2, True)
+        quant_w(0)
+        make_tp(1)
+        gather_v(3, True)
+        quant_v(1)
+        quant_v(0)
+        quant_v(2)
+        quant_v(3)
+        weights(1)
+        quant_w(1)
+        out_rows = out_0.rearrange("(p r) q -> p r q", r=PACK)
+        words_out = out_1[0].rearrange("p c r -> p (c r)").bitcast(I32)
+        oc = sb.tile([P, Q], U32, name="oc", align_bytes=64)
+        osc = sb.tile([P, Q], U8, name="osc", align_bytes=64)
+        for h in range(QT):
+            cols = slice(h * P, (h + 1) * P)
+            for r in range(PACK):
+                product(r, h)
+            o16 = sb.tile([P, P, PACK], BF16, name="o16_%d" % h, align_bytes=64)
+            o32 = sb.tile([P, PACK, P], F32, name="o32_%d" % h)
+            if h == 0:
+                nc.scalar.copy(out=o16[:], in_=ob[h][:].rearrange("p r q -> p q r"))
+            else:
+                nc.vector.tensor_copy(out=o16[:], in_=ob[h][:].rearrange("p r q -> p q r"))
+            nc.scalar.copy(out=o32[:], in_=ob[h][:])
+            nc.vector.quantize_mx(out=oc[:, cols].bitcast(FP8X4), scales=osc[:, cols], in_=o16[:].rearrange("p q r -> p (q r)"))
+            nc.sync.dma_start(out=out_rows[:, :, cols], in_=o32[:])
+        nc.sync.dma_start(out=words_out, in_=oc[:].bitcast(I32))
+        for g in range(4):
+            eng = nc.sync if g % 2 == 0 else nc.scalar
+            eng.dma_start(out=out_2[0, 4 * g : 4 * g + 4, :].bitcast(I32), in_=osc[32 * g : 32 * g + 4, :].bitcast(I32))

@@ -24,11 +24,11 @@ QT = Q // P
 
 
 def dealt(bank):
-    return bank[:].rearrange("p (s j) -> p j s", j=PACK)
+    return bank[:].rearrange("p (s u e) -> p u s e", u=2, e=2)
 
 
 def by_place(tile):
-    return tile[:].rearrange("p (j s) -> p j s", j=PACK)
+    return tile[:].rearrange("p (u s e) -> p u s e", u=2, e=2)
 
 
 def tile_attend_ttproductscore_pl_kernel(tc, query, dquery, query2, dquery2, keys_words, keys_scales, slot_factor, vals, offs, out_0, out_1, out_2):
@@ -52,9 +52,9 @@ def tile_attend_ttproductscore_pl_kernel(tc, query, dquery, query2, dquery2, key
         nc.scalar.dma_start(out=os4[:, 0, :], in_=slot_factor.rearrange("o (s j) -> (o s) j", j=PACK))
         warm2 = sb.tile([P, 1], F32, name="warm2")
         nc.scalar.activation(out=warm2[:], in_=ident[:, 0:1], func=ACT.Exp)
-        names = ("a", "b", "ta", "tb")
+        names = ("b", "a", "ta", "tb")
         raw = {}
-        for n, src in zip(names, (query, query2, dquery, dquery2)):
+        for n, src in zip(names, (query2, query, dquery, dquery2)):
             raw[n] = sb.tile([P, PACK, Q], F32, name="raw_" + n)
             nc.sync.dma_start(out=raw[n][:], in_=src.rearrange("(p j) w -> p j w", j=PACK))
         vwin = []
@@ -123,7 +123,7 @@ def tile_attend_ttproductscore_pl_kernel(tc, query, dquery, query2, dquery2, key
             nc.scalar.activation(out=by_place(b1[h]), in_=dealt(bank["b", h]), func=ACT.Copy, bias=1.0)
 
         def make_s(h):
-            nc.vector.scalar_tensor_tensor(out=by_place(s[h]), in0=dealt(bank["b", h]), scalar=1.0, in1=by_place(a_sb[h]), op0=ALU.add, op1=ALU.mult)
+            nc.vector.tensor_tensor(out=by_place(s[h]), in0=dealt(bank["a", h]), in1=by_place(b1[h]), op=ALU.mult)
 
         def make_max(h):
             nc.vector.tensor_reduce(out=negmax[h][:], in_=s[h][:], axis=AX.X, op=ALU.max, negate=True)
@@ -150,7 +150,7 @@ def tile_attend_ttproductscore_pl_kernel(tc, query, dquery, query2, dquery2, key
             nc.scalar.activation(out=z[h][:], in_=p[h][:], func=ACT.Copy, scale=k[h][:])
             t = ps.tile([P, PACK, P], F32, name="wT%d" % h, tag="bank_ta%d" % h)
             for j in range(PACK):
-                cols = slice(j * P, (j + 1) * P)
+                cols = slice((j // 2) * 2 * P + j % 2, (j // 2 + 1) * 2 * P, 2)
                 nc.tensor.matmul(out=t[:, j, :], lhsT=tp[h][:, cols], rhs=ident[:], start=True, stop=False, is_transpose=True)
                 nc.tensor.matmul(out=t[:, j, :], lhsT=z[h][:, cols], rhs=ident[:], start=False, stop=True, is_transpose=True)
             wT[h] = t
@@ -161,14 +161,15 @@ def tile_attend_ttproductscore_pl_kernel(tc, query, dquery, query2, dquery2, key
                 nc.vector.tensor_copy(g[:], vwin[r][:].indirect(offsets[:]))
             else:
                 w16 = sb.tile([P, T], BF16, name="vwin16_%d" % r, align_bytes=64)
-                nc.scalar.activation(out=w16[:], in_=vwin[r][:], func=ACT.Copy)
+                for piece in range(4):
+                    nc.scalar.activation(out=w16[:, piece * I : (piece + 1) * I], in_=vwin[r][:, piece * I : (piece + 1) * I], func=ACT.Copy)
                 nc.scalar.activation(out=g[:], in_=w16[:].indirect(offsets[:]), func=ACT.Copy)
             words = g[:].bitcast(F32)
-            t = ps.tile([P, 2, P], F32, name="vT%d" % r, tag="bank_a%d" % (r % 2))
+            t = ps.tile([P, 2, P], F32, name="vT%d" % r, tag="bank_b%d" % (r % 2))
             for half in range(2):
                 nc.tensor.transpose(t[:, half, :], words[:, half : I // 2 : 2], ident[:])
             vb[r] = sb.tile([P, P * PACK], BF16, name="vb%d" % r, align_bytes=64)
-            nc.scalar.copy(out=vb[r][:].bitcast(F32).rearrange("p (e u) -> p e u", u=2), in_=t[:].rearrange("p u e -> p e u"))
+            nc.scalar.copy(out=vb[r][:].bitcast(F32).rearrange("p (c i u) -> p c u i", u=2, i=2), in_=t[:].rearrange("p u (c i) -> p c u i", i=2))
 
         def quant_v(r):
             vc[r] = sb.tile([P, P], U32, name="vc%d" % r, align_bytes=64)
@@ -177,7 +178,7 @@ def tile_attend_ttproductscore_pl_kernel(tc, query, dquery, query2, dquery2, key
 
         def weights(h):
             wb[h] = sb.tile([P, P, PACK], BF16, name="wb%d" % h, align_bytes=64)
-            nc.vector.tensor_tensor(out=wb[h][:], in0=wT[h][:].rearrange("p j q -> p q j"), in1=os4[:].to_broadcast([P, P, PACK]), op=ALU.mult)
+            nc.vector.tensor_tensor(out=wb[h][:].rearrange("p (c i) j -> p c j i", i=2), in0=wT[h][:].rearrange("p j (c i) -> p c j i", i=2), in1=os4[:].unsqueeze(3).to_broadcast([P, P // 2, PACK, 2]), op=ALU.mult)
 
         def quant_w(h):
             wc[h] = sb.tile([P, P], U32, name="wc%d" % h, align_bytes=64)
@@ -188,25 +189,25 @@ def tile_attend_ttproductscore_pl_kernel(tc, query, dquery, query2, dquery2, key
 
         def product(r, h):
             if h not in ob:
-                ob[h] = ps.tile([P, PACK, P], F32, name="o%d" % h, tag="bank_b%d" % h)
+                ob[h] = ps.tile([P, PACK, P], F32, name="o%d" % h, tag="bank_a%d" % h)
             nc.tensor.matmul_mx(out=ob[h][:, r, :], lhsT=vc[r][:].bitcast(FP8X4), lhsT_scale=vs[r][:],
                                 rhs=wc[h][:].bitcast(FP8X4), rhs_scale=ws[h][:], start=True, stop=True)
 
-        weave("a", 0, 1, False)
-        weave("a", 1, 2, False)
-        quant_q("a", 0, 1)
-        weave("b", 0, 1, True)
+        weave("b", 0, 1, False)
         weave("b", 1, 2, False)
-        quant_q("a", 1, 2)
         quant_q("b", 0, 1)
-        score("a", 0)
-        score("b", 0)
+        weave("a", 0, 1, True)
+        weave("a", 1, 2, False)
         quant_q("b", 1, 2)
-        score("a", 1)
+        quant_q("a", 0, 1)
+        score("b", 0)
+        score("a", 0)
+        quant_q("a", 1, 2)
         score("b", 1)
-        copy_a(0)
+        score("a", 1)
+        copy_b(0)
         weave("ta", 0, 2, True)
-        copy_a(1)
+        copy_b(1)
         make_s(0)
         quant_q("ta", 0, 2)
         weave("tb", 0, 2, False)
@@ -218,16 +219,16 @@ def tile_attend_ttproductscore_pl_kernel(tc, query, dquery, query2, dquery2, key
         score("tb", 0)
         score("tb", 1)
         make_max(1)
-        copy_b(0)
         make_p(0)
-        copy_b(1)
+        copy_a(0)
         make_p(1)
-        make_v(0)
+        copy_a(1)
         make_u(0)
+        make_v(0)
         make_rz(0)
-        make_v(1)
-        make_ts(0, nc.vector)
         make_u(1)
+        make_ts(0, nc.vector)
+        make_v(1)
         make_tp(0)
         make_rz(1)
         make_ts(1, nc.vector)
@@ -255,9 +256,9 @@ def tile_attend_ttproductscore_pl_kernel(tc, query, dquery, query2, dquery2, key
             o16 = sb.tile([P, P, PACK], BF16, name="o16_%d" % h, align_bytes=64)
             o32 = sb.tile([P, PACK, P], F32, name="o32_%d" % h)
             if h == 0:
-                nc.scalar.copy(out=o16[:], in_=ob[h][:].rearrange("p r q -> p q r"))
+                nc.scalar.copy(out=o16[:].rearrange("p (c i) r -> p c r i", i=2), in_=ob[h][:].rearrange("p r (c i) -> p c r i", i=2))
             else:
-                nc.vector.tensor_copy(out=o16[:], in_=ob[h][:].rearrange("p r q -> p q r"))
+                nc.vector.tensor_copy(out=o16[:].rearrange("p (c i) r -> p c r i", i=2), in_=ob[h][:].rearrange("p r (c i) -> p c r i", i=2))
             nc.scalar.copy(out=o32[:], in_=ob[h][:])
             nc.vector.quantize_mx(out=oc[:, cols].bitcast(FP8X4), scales=osc[:, cols], in_=o16[:].rearrange("p q r -> p (q r)"))
             nc.sync.dma_start(out=out_rows[:, :, cols], in_=o32[:])

@@ -21,6 +21,7 @@ AX = mybir.AxisListType
 P = 128
 PACK = 4
 QT = Q // P
+SHARE = {"ts1":"vwin1","tp1":"vwin2","vg3":"vwin1","wb0":"vwin3"}
 
 
 def dealt(bank):
@@ -40,18 +41,20 @@ def tile_attend_ttproductscore_pl_kernel(tc, query, dquery, query2, dquery2, key
         offsets = sb.tile([P, I // 16], U16, name="offsets")
         kw = sb.tile([P, T], U16, name="kw", align_bytes=64)
         ks = sb.tile([P, T], U8, name="ks", align_bytes=64)
-        nc.gpsimd.memset(ks[:].bitcast(I32), 0)
+        warm = sb.tile([P, 1], F32, name="warm")
+        nc.vector.memset(ks[:].bitcast(I32), 0)
+        nc.vector.memset(warm[:], 0.0)
         ident = sb.tile([P, P], F32, name="ident")
         make_identity(nc, ident[:])
 
         nc.sync.dma_start(offsets[:], offs)
-        for g in range(4):
-            nc.scalar.dma_start(out=ks[32 * g : 32 * g + 4, :].bitcast(I32), in_=keys_scales[0, 4 * g : 4 * g + 4, :].bitcast(I32))
         nc.sync.dma_start(out=kw[:].bitcast(I32), in_=keys_words[0].bitcast(I32))
+        for g in range(4):
+            nc.sync.dma_start(out=ks[32 * g : 32 * g + 4, :].bitcast(I32), in_=keys_scales[0, 4 * g : 4 * g + 4, :].bitcast(I32))
         os4 = sb.tile([P, 1, PACK], F32, name="os4")
         nc.scalar.dma_start(out=os4[:, 0, :], in_=slot_factor.rearrange("o (s j) -> (o s) j", j=PACK))
         warm2 = sb.tile([P, 1], F32, name="warm2")
-        nc.scalar.activation(out=warm2[:], in_=ident[:, 0:1], func=ACT.Exp)
+        nc.scalar.activation(out=warm2[:], in_=warm[:], func=ACT.Exp)
         names = ("b", "a", "ta", "tb")
         raw = {}
         for n, src in zip(names, (query2, query, dquery, dquery2)):
@@ -59,23 +62,48 @@ def tile_attend_ttproductscore_pl_kernel(tc, query, dquery, query2, dquery2, key
             nc.sync.dma_start(out=raw[n][:], in_=src.rearrange("(p j) w -> p j w", j=PACK))
         vwin = []
         for r in range(PACK):
-            w = sb.tile([P, T], F32, name="vwin%d" % r)
+            w = sb.tile([P, T], F32, name="vwin%d" % r, tag="vwin%d" % r, align_bytes=64)
             nc.sync.dma_start(out=w[:], in_=vals.rearrange("(p r) t -> r p t", r=PACK)[r])
             vwin.append(w)
 
         kwg = sb.tile([P, I], U16, name="kwg", align_bytes=64)
         ksg = sb.tile([P, I], U8, name="ksg", align_bytes=64)
-        nc.vector.tensor_copy(ksg[:], ks[:].indirect(offsets[:]))
         nc.vector.tensor_copy(kwg[:], kw[:].indirect(offsets[:]))
+        nc.vector.tensor_copy(ksg[:], ks[:].indirect(offsets[:]))
 
         qb, qc, qs, bank = {}, {}, {}, {}
 
+        pair = sb.tile([P, Q, PACK], BF16, name="pair", align_bytes=64)
+
+        def quant_pair():
+            cd = sb.tile([P, Q], U32, name="qc_pair", align_bytes=64)
+            sc = sb.tile([P, Q], U8, name="qs_pair", align_bytes=64)
+            nc.vector.quantize_mx(out=cd[:].bitcast(FP8X4), scales=sc[:], in_=pair[:].rearrange("p w j -> p (w j)"))
+            for m, n in enumerate(("b", "a")):
+                qc[n, 1] = cd[:, m * P : (m + 1) * P]
+                qs[n, 1] = sc[:, m * P : (m + 1) * P]
+
+        vpair = [sb.tile([P, 2 * I], BF16, name="vpair%d" % m, align_bytes=64) for m in range(2)]
+
+        def quant_v2(r, r2):
+            cd = sb.tile([P, Q], U32, name="vc%d" % r, align_bytes=64)
+            sc = sb.tile([P, Q], U8, name="vs%d" % r, align_bytes=64)
+            nc.vector.quantize_mx(out=cd[:].bitcast(FP8X4), scales=sc[:], in_=vpair[r // 2][:])
+            for m, n in enumerate((r, r2)):
+                vc[n] = cd[:, m * P : (m + 1) * P]
+                vs[n] = sc[:, m * P : (m + 1) * P]
+
         def weave(n, h0, h1, on_vector):
             width = (h1 - h0) * P
-            g = sb.tile([P, width, PACK], BF16, name="qb_%s%d" % (n, h0), align_bytes=64)
+            if h0 == 1:
+                g = pair[:, (0 if n == "b" else P) : (P if n == "b" else Q), :]
+            else:
+                g = sb.tile([P, width, PACK], BF16, name="qb_%s%d" % (n, h0), align_bytes=64)
             dst = g[:].rearrange("p (c i) t -> p c t i", i=4)
             src = raw[n][:, :, h0 * P : h1 * P].rearrange("p t (c i) -> p c t i", i=4)
-            if on_vector:
+            if on_vector == "g":
+                nc.gpsimd.tensor_scalar(out=dst, in0=src, scalar1=1.0, scalar2=0.0, op0=ALU.mult, op1=ALU.add)
+            elif on_vector:
                 nc.vector.tensor_copy(out=dst, in_=src)
             else:
                 nc.scalar.copy(out=dst, in_=src)
@@ -97,7 +125,7 @@ def tile_attend_ttproductscore_pl_kernel(tc, query, dquery, query2, dquery2, key
                                 rhs=kwg[:].bitcast(FP4X4), rhs_scale=ksg[:], start=True, stop=True)
 
         def f32tile(name, cols=I):
-            return sb.tile([P, cols], F32, name=name)
+            return sb.tile([P, cols], F32, name=name, tag=SHARE.get(name, name), align_bytes=64)
 
         a_sb = [f32tile("a_sb%d" % h) for h in range(QT)]
         b1 = [f32tile("b1_%d" % h) for h in range(QT)]
@@ -147,16 +175,17 @@ def tile_attend_ttproductscore_pl_kernel(tc, query, dquery, query2, dquery2, key
         def make_tp(h):
             nc.vector.scalar_tensor_tensor(out=tp[h][:], in0=ts[h][:], scalar=rz[h][:], in1=p[h][:], op0=ALU.mult, op1=ALU.mult, accum_out=c[h][:])
             nc.scalar.activation(out=k[h][:], in_=c[h][:], func=ACT.Copy, scale=nrz[h][:])
-            nc.scalar.activation(out=z[h][:], in_=p[h][:], func=ACT.Copy, scale=k[h][:])
+            nc.scalar.activation(out=z[h][:].rearrange("p (u e s) -> p u s e", u=2, e=2), in_=by_place(p[h]), func=ACT.Copy, scale=k[h][:])
             t = ps.tile([P, PACK, P], F32, name="wT%d" % h, tag="bank_ta%d" % h)
             for j in range(PACK):
                 cols = slice((j // 2) * 2 * P + j % 2, (j // 2 + 1) * 2 * P, 2)
-                nc.tensor.matmul(out=t[:, j, :], lhsT=tp[h][:, cols], rhs=ident[:], start=True, stop=False, is_transpose=True)
-                nc.tensor.matmul(out=t[:, j, :], lhsT=z[h][:, cols], rhs=ident[:], start=False, stop=True, is_transpose=True)
+                nc.tensor.matmul(out=t[:, j, :], lhsT=tp[h][:, cols], rhs=ident[:], start=(j == 0), stop=False, is_transpose=True)
+            for j in range(PACK):
+                nc.tensor.matmul(out=t[:, j, :], lhsT=z[h][:, j * P : (j + 1) * P], rhs=ident[:], start=False, stop=(j == PACK - 1), is_transpose=True)
             wT[h] = t
 
         def gather_v(r, on_vector):
-            g = sb.tile([P, I], BF16, name="vg%d" % r, align_bytes=64)
+            g = sb.tile([P, I], BF16, name="vg%d" % r, tag=SHARE.get("vg%d" % r, "vg%d" % r), align_bytes=64)
             if on_vector:
                 nc.vector.tensor_copy(g[:], vwin[r][:].indirect(offsets[:]))
             else:
@@ -168,8 +197,8 @@ def tile_attend_ttproductscore_pl_kernel(tc, query, dquery, query2, dquery2, key
             t = ps.tile([P, 2, P], F32, name="vT%d" % r, tag="bank_b%d" % (r % 2))
             for half in range(2):
                 nc.tensor.transpose(t[:, half, :], words[:, half : I // 2 : 2], ident[:])
-            vb[r] = sb.tile([P, P * PACK], BF16, name="vb%d" % r, align_bytes=64)
-            nc.scalar.copy(out=vb[r][:].bitcast(F32).rearrange("p (c i u) -> p c u i", u=2, i=2), in_=t[:].rearrange("p u (c i) -> p c u i", i=2))
+            vb[r] = vpair[r // 2][:, (r % 2) * I : (r % 2 + 1) * I]
+            nc.scalar.copy(out=vb[r].bitcast(F32).rearrange("p (c i u) -> p c u i", u=2, i=2), in_=t[:].rearrange("p u (c i) -> p c u i", i=2))
 
         def quant_v(r):
             vc[r] = sb.tile([P, P], U32, name="vc%d" % r, align_bytes=64)
@@ -177,7 +206,7 @@ def tile_attend_ttproductscore_pl_kernel(tc, query, dquery, query2, dquery2, key
             nc.vector.quantize_mx(out=vc[r][:].bitcast(FP8X4), scales=vs[r][:], in_=vb[r][:])
 
         def weights(h):
-            wb[h] = sb.tile([P, P, PACK], BF16, name="wb%d" % h, align_bytes=64)
+            wb[h] = sb.tile([P, P, PACK], BF16, name="wb%d" % h, tag=SHARE.get("wb%d" % h, "wb%d" % h), align_bytes=64)
             nc.vector.tensor_tensor(out=wb[h][:].rearrange("p (c i) j -> p c j i", i=2), in0=wT[h][:].rearrange("p j (c i) -> p c j i", i=2), in1=os4[:].unsqueeze(3).to_broadcast([P, P // 2, PACK, 2]), op=ALU.mult)
 
         def quant_w(h):
@@ -190,79 +219,81 @@ def tile_attend_ttproductscore_pl_kernel(tc, query, dquery, query2, dquery2, key
         def product(r, h):
             if h not in ob:
                 ob[h] = ps.tile([P, PACK, P], F32, name="o%d" % h, tag="bank_a%d" % h)
-            nc.tensor.matmul_mx(out=ob[h][:, r, :], lhsT=vc[r][:].bitcast(FP8X4), lhsT_scale=vs[r][:],
+            nc.tensor.matmul_mx(out=ob[h][:, r, :], lhsT=vc[r].bitcast(FP8X4), lhsT_scale=vs[r],
                                 rhs=wc[h][:].bitcast(FP8X4), rhs_scale=ws[h][:], start=True, stop=True)
 
         weave("b", 0, 1, False)
         weave("b", 1, 2, False)
         quant_q("b", 0, 1)
         weave("a", 0, 1, True)
-        weave("a", 1, 2, False)
-        quant_q("b", 1, 2)
         quant_q("a", 0, 1)
         score("b", 0)
         score("a", 0)
-        quant_q("a", 1, 2)
+        weave("a", 1, 2, False)
+        quant_pair()
         score("b", 1)
         score("a", 1)
         copy_b(0)
-        weave("ta", 0, 2, True)
         copy_b(1)
         make_s(0)
-        quant_q("ta", 0, 2)
-        weave("tb", 0, 2, False)
+        weave("ta", 0, 2, True)
         make_s(1)
         make_max(0)
+        quant_q("ta", 0, 2)
+        make_max(1)
         score("ta", 0)
         score("ta", 1)
+        weave("tb", 0, 2, False)
         quant_q("tb", 0, 2)
         score("tb", 0)
         score("tb", 1)
-        make_max(1)
         make_p(0)
         copy_a(0)
         make_p(1)
         copy_a(1)
         make_u(0)
         make_v(0)
-        make_rz(0)
         make_u(1)
-        make_ts(0, nc.vector)
+        make_rz(0)
         make_v(1)
-        make_tp(0)
+        make_ts(0, nc.vector)
         make_rz(1)
-        make_ts(1, nc.vector)
+        make_tp(0)
         gather_v(0, False)
         gather_v(1, True)
-        weights(0)
+        make_ts(1, nc.vector)
         gather_v(2, True)
-        quant_w(0)
         make_tp(1)
         gather_v(3, True)
-        quant_v(1)
-        quant_v(0)
-        quant_v(2)
-        quant_v(3)
+        weights(0)
+        quant_v2(0, 1)
+        quant_w(0)
+        quant_v2(2, 3)
         weights(1)
         quant_w(1)
         out_rows = out_0.rearrange("(p r) q -> p r q", r=PACK)
         words_out = out_1[0].rearrange("p c r -> p (c r)").bitcast(I32)
         oc = sb.tile([P, Q], U32, name="oc", align_bytes=64)
         osc = sb.tile([P, Q], U8, name="osc", align_bytes=64)
-        for h in range(QT):
-            cols = slice(h * P, (h + 1) * P)
-            for r in range(PACK):
-                product(r, h)
-            o16 = sb.tile([P, P, PACK], BF16, name="o16_%d" % h, align_bytes=64)
-            o32 = sb.tile([P, PACK, P], F32, name="o32_%d" % h)
-            if h == 0:
-                nc.scalar.copy(out=o16[:].rearrange("p (c i) r -> p c r i", i=2), in_=ob[h][:].rearrange("p r (c i) -> p c r i", i=2))
-            else:
-                nc.vector.tensor_copy(out=o16[:].rearrange("p (c i) r -> p c r i", i=2), in_=ob[h][:].rearrange("p r (c i) -> p c r i", i=2))
-            nc.scalar.copy(out=o32[:], in_=ob[h][:])
-            nc.vector.quantize_mx(out=oc[:, cols].bitcast(FP8X4), scales=osc[:, cols], in_=o16[:].rearrange("p q r -> p (q r)"))
-            nc.sync.dma_start(out=out_rows[:, :, cols], in_=o32[:])
-        nc.sync.dma_start(out=words_out, in_=oc[:].bitcast(I32))
+        o16 = [sb.tile([P, P, PACK], BF16, name="o16_%d" % h, align_bytes=64) for h in range(QT)]
+        o32 = [sb.tile([P, PACK, P], F32, name="o32_%d" % h) for h in range(QT)]
+        for r in range(PACK):
+            product(r, 0)
+        nc.scalar.copy(out=o32[0][:], in_=ob[0][:])
+        nc.sync.dma_start(out=out_rows[:, :, 0:P], in_=o32[0][:])
+        nc.scalar.copy(out=o16[0][:].rearrange("p (c i) r -> p c r i", i=2), in_=ob[0][:].rearrange("p r (c i) -> p c r i", i=2))
+        nc.vector.quantize_mx(out=oc[:, 0:P].bitcast(FP8X4), scales=osc[:, 0:P], in_=o16[0][:].rearrange("p q r -> p (q r)"))
+        nc.sync.dma_start(out=words_out[:, 0:P], in_=oc[:, 0:P].bitcast(I32))
+        halves = [ps.tile([P, 2, P], F32, name="o1_%d" % n, tag=tag) for n, tag in enumerate(("bank_a1", "bank_tb1"))]
+        for r in range(PACK):
+            nc.tensor.matmul_mx(out=halves[r // 2][:, r % 2, :], lhsT=vc[r].bitcast(FP8X4), lhsT_scale=vs[r],
+                                rhs=wc[1][:].bitcast(FP8X4), rhs_scale=ws[1][:], start=True, stop=True)
+        nc.scalar.copy(out=o32[1][:, 0:2, :], in_=halves[0][:])
+        nc.vector.tensor_copy(out=o32[1][:, 2:4, :], in_=halves[1][:])
+        nc.sync.dma_start(out=out_rows[:, :, P:Q], in_=o32[1][:])
+        nc.vector.tensor_copy(out=o16[1][:].rearrange("p (c i) r -> p c r i", i=4), in_=o32[1][:].rearrange("p r (c i) -> p c r i", i=4))
+        nc.vector.quantize_mx(out=oc[:, P:Q].bitcast(FP8X4), scales=osc[:, P:Q], in_=o16[1][:].rearrange("p q r -> p (q r)"))
+        nc.sync.dma_start(out=words_out[:, P:Q], in_=oc[:, P:Q].bitcast(I32))
         for g in range(4):
-            eng = nc.sync if g % 2 == 0 else nc.scalar
+            eng = nc.scalar if g % 2 == 0 else nc.sync
             eng.dma_start(out=out_2[0, 4 * g : 4 * g + 4, :].bitcast(I32), in_=osc[32 * g : 32 * g + 4, :].bitcast(I32))

from contextlib import ExitStack

import concourse.mybir as mybir
from concourse.masks import make_identity

D, E, T, I, Q = 512, 512, 2048, 512, 256
FLOPS = 4 * 2 * Q * D * I + 2 * E * I * Q

F32 = mybir.dt.float32
BF16 = mybir.dt.bfloat16
I32 = mybir.dt.int32
U32 = mybir.dt.uint32
U16 = mybir.dt.uint16
U8 = mybir.dt.uint8
FP8X4 = mybir.dt.float8_e4m3fn_x4
FP4X4 = mybir.dt.float4_e2m1fn_x4
ALU = mybir.AluOpType
ACT = mybir.ActivationFunctionType
AX = mybir.AxisListType

P = 128
PACK = 4
QT = Q // P
SHARE = {"ts1":"vwin1","tp1":"vwin2","vg3":"vwin1","wb0":"vwin3"}


def dealt(bank):
    return bank[:].rearrange("p (s u e) -> p u s e", u=2, e=2)


def by_place(tile):
    return tile[:].rearrange("p (u s e) -> p u s e", u=2, e=2)


def tile_attend_ttproductscore_pl_kernel(tc, query, dquery, query2, dquery2, keys_words, keys_scales, slot_factor, vals, offs, out_0, out_1, out_2):
    nc = tc.nc
    with ExitStack() as ctx:
        sb = ctx.enter_context(tc.tile_pool(name="sb", bufs=1))
        ps = ctx.enter_context(tc.psum_pool(name="ps", bufs=1))

        offsets = sb.tile([P, I // 16], U16, name="offsets")
        kw = sb.tile([P, T], U16, name="kw", align_bytes=64)
        ks = sb.tile([P, T], U8, name="ks", align_bytes=64)
        warm = sb.tile([P, 1], F32, name="warm")
        nc.vector.memset(ks[:].bitcast(I32), 0)
        nc.vector.memset(warm[:], 0.0)
        ident = sb.tile([P, P], F32, name="ident")
        make_identity(nc, ident[:])

        nc.sync.dma_start(offsets[:], offs)
        nc.sync.dma_start(out=kw[:].bitcast(I32), in_=keys_words[0].bitcast(I32))
        for g in range(4):
            nc.sync.dma_start(out=ks[32 * g : 32 * g + 4, :].bitcast(I32), in_=keys_scales[0, 4 * g : 4 * g + 4, :].bitcast(I32))
        os4 = sb.tile([P, 1, PACK], F32, name="os4")
        nc.scalar.dma_start(out=os4[:, 0, :], in_=slot_factor.rearrange("o (s j) -> (o s) j", j=PACK))
        warm2 = sb.tile([P, 1], F32, name="warm2")
        nc.scalar.activation(out=warm2[:], in_=warm[:], func=ACT.Exp)
        names = ("b", "a", "ta", "tb")
        raw = {}
        for n, src in zip(names, (query2, query, dquery, dquery2)):
            raw[n] = sb.tile([P, PACK, Q], F32, name="raw_" + n)
            nc.sync.dma_start(out=raw[n][:], in_=src.rearrange("(p j) w -> p j w", j=PACK))
        vwin = []
        for r in range(PACK):
            w = sb.tile([P, T], F32, name="vwin%d" % r, tag="vwin%d" % r, align_bytes=64)
            nc.sync.dma_start(out=w[:], in_=vals.rearrange("(p r) t -> r p t", r=PACK)[r])
            vwin.append(w)

        kwg = sb.tile([P, I], U16, name="kwg", align_bytes=64)
        ksg = sb.tile([P, I], U8, name="ksg", align_bytes=64)
        nc.vector.tensor_copy(kwg[:], kw[:].indirect(offsets[:]))
        nc.vector.tensor_copy(ksg[:], ks[:].indirect(offsets[:]))

        qb, qc, qs, bank = {}, {}, {}, {}

        pair = sb.tile([P, Q, PACK], BF16, name="pair", align_bytes=64)

        def quant_pair():
            cd = sb.tile([P, Q], U32, name="qc_pair", align_bytes=64)
            sc = sb.tile([P, Q], U8, name="qs_pair", align_bytes=64)
            nc.vector.quantize_mx(out=cd[:].bitcast(FP8X4), scales=sc[:], in_=pair[:].rearrange("p w j -> p (w j)"))
            for m, n in enumerate(("b", "a")):
                qc[n, 1] = cd[:, m * P : (m + 1) * P]
                qs[n, 1] = sc[:, m * P : (m + 1) * P]

        vpair = [sb.tile([P, 2 * I], BF16, name="vpair%d" % m, align_bytes=64) for m in range(2)]

        def quant_v2(r, r2):
            cd = sb.tile([P, Q], U32, name="vc%d" % r, align_bytes=64)
            sc = sb.tile([P, Q], U8, name="vs%d" % r, align_bytes=64)
            nc.vector.quantize_mx(out=cd[:].bitcast(FP8X4), scales=sc[:], in_=vpair[r // 2][:])
            for m, n in enumerate((r, r2)):
                vc[n] = cd[:, m * P : (m + 1) * P]
                vs[n] = sc[:, m * P : (m + 1) * P]

        def weave(n, h0, h1, on_vector):
            width = (h1 - h0) * P
            if h0 == 1:
                g = pair[:, (0 if n == "b" else P) : (P if n == "b" else Q), :]
            else:
                g = sb.tile([P, width, PACK], BF16, name="qb_%s%d" % (n, h0), align_bytes=64)
            dst = g[:].rearrange("p (c i) t -> p c t i", i=4)
            src = raw[n][:, :, h0 * P : h1 * P].rearrange("p t (c i) -> p c t i", i=4)
            if on_vector == "g":
                nc.gpsimd.tensor_scalar(out=dst, in0=src, scalar1=1.0, scalar2=0.0, op0=ALU.mult, op1=ALU.add)
            elif on_vector:
                nc.vector.tensor_copy(out=dst, in_=src)
            else:
                nc.scalar.copy(out=dst, in_=src)
            qb[n, h0] = g

        def quant_q(n, h0, h1):
            width = (h1 - h0) * P
            cd = sb.tile([P, width], U32, name="qc_%s%d" % (n, h0), align_bytes=64)
            sc = sb.tile([P, width], U8, name="qs_%s%d" % (n, h0), align_bytes=64)
            nc.vector.quantize_mx(out=cd[:].bitcast(FP8X4), scales=sc[:], in_=qb[n, h0][:].rearrange("p w j -> p (w j)"))
            for h in range(h0, h1):
                cols = slice((h - h0) * P, (h - h0 + 1) * P)
                qc[n, h] = cd[:, cols]
                qs[n, h] = sc[:, cols]

        def score(n, h):
            bank[n, h] = ps.tile([P, I], F32, name="s_%s%d" % (n, h), tag="bank_%s%d" % (n, h))
            nc.tensor.matmul_mx(out=bank[n, h][:], lhsT=qc[n, h].bitcast(FP8X4), lhsT_scale=qs[n, h],
                                rhs=kwg[:].bitcast(FP4X4), rhs_scale=ksg[:], start=True, stop=True)

        def f32tile(name, cols=I):
            return sb.tile([P, cols], F32, name=name, tag=SHARE.get(name, name), align_bytes=64)

        a_sb = [f32tile("a_sb%d" % h) for h in range(QT)]
        b1 = [f32tile("b1_%d" % h) for h in range(QT)]
        s = [f32tile("s%d" % h) for h in range(QT)]
        p = [f32tile("p%d" % h) for h in range(QT)]
        u = [f32tile("u%d" % h) for h in range(QT)]
        v = [f32tile("v%d" % h) for h in range(QT)]
        ts = [f32tile("ts%d" % h) for h in range(QT)]
        tp = [f32tile("tp%d" % h) for h in range(QT)]
        z = [f32tile("z%d" % h) for h in range(QT)]
        negmax = [f32tile("negmax%d" % h, 1) for h in range(QT)]
        zsum = [f32tile("zsum%d" % h, 1) for h in range(QT)]
        rz = [f32tile("rz%d" % h, 1) for h in range(QT)]
        nrz = [f32tile("nrz%d" % h, 1) for h in range(QT)]
        c = [f32tile("c%d" % h, 1) for h in range(QT)]
        k = [f32tile("k%d" % h, 1) for h in range(QT)]
        wT, wb, wc, ws, vg, vb, vc, vs = {}, {}, {}, {}, {}, {}, {}, {}

        def copy_a(h):
            nc.scalar.copy(out=by_place(a_sb[h]), in_=dealt(bank["a", h]))

        def copy_b(h):
            nc.scalar.activation(out=by_place(b1[h]), in_=dealt(bank["b", h]), func=ACT.Copy, bias=1.0)

        def make_s(h):
            nc.vector.tensor_tensor(out=by_place(s[h]), in0=dealt(bank["a", h]), in1=by_place(b1[h]), op=ALU.mult)

        def make_max(h):
            nc.vector.tensor_reduce(out=negmax[h][:], in_=s[h][:], axis=AX.X, op=ALU.max, negate=True)

        def make_p(h):
            nc.scalar.activation(out=p[h][:], in_=s[h][:], func=ACT.Exp, bias=negmax[h][:], accum_out=zsum[h][:])

        def make_u(h):
            nc.vector.tensor_tensor(out=by_place(u[h]), in0=dealt(bank["ta", h]), in1=by_place(b1[h]), op=ALU.mult)

        def make_v(h):
            nc.vector.tensor_tensor(out=by_place(v[h]), in0=dealt(bank["tb", h]), in1=by_place(a_sb[h]), op=ALU.mult)

        def make_rz(h):
            nc.vector.reciprocal(out=rz[h][:], in_=zsum[h][:])
            nc.scalar.activation(out=nrz[h][:], in_=rz[h][:], func=ACT.Copy, scale=-1.0)

        def make_ts(h, eng):
            eng.tensor_tensor(out=ts[h][:], in0=u[h][:], in1=v[h][:], op=ALU.add)

        def make_tp(h):
            nc.vector.scalar_tensor_tensor(out=tp[h][:], in0=ts[h][:], scalar=rz[h][:], in1=p[h][:], op0=ALU.mult, op1=ALU.mult, accum_out=c[h][:])
            nc.scalar.activation(out=k[h][:], in_=c[h][:], func=ACT.Copy, scale=nrz[h][:])
            nc.scalar.activation(out=z[h][:].rearrange("p (u e s) -> p u s e", u=2, e=2), in_=by_place(p[h]), func=ACT.Copy, scale=k[h][:])
            t = ps.tile([P, PACK, P], F32, name="wT%d" % h, tag="bank_ta%d" % h)
            for j in range(PACK):
                cols = slice((j // 2) * 2 * P + j % 2, (j // 2 + 1) * 2 * P, 2)
                nc.tensor.matmul(out=t[:, j, :], lhsT=tp[h][:, cols], rhs=ident[:], start=(j == 0), stop=False, is_transpose=True)
            for j in range(PACK):
                nc.tensor.matmul(out=t[:, j, :], lhsT=z[h][:, j * P : (j + 1) * P], rhs=ident[:], start=False, stop=(j == PACK - 1), is_transpose=True)
            wT[h] = t

        def gather_v(r, on_vector):
            g = sb.tile([P, I], BF16, name="vg%d" % r, tag=SHARE.get("vg%d" % r, "vg%d" % r), align_bytes=64)
            if on_vector:
                nc.vector.tensor_copy(g[:], vwin[r][:].indirect(offsets[:]))
            else:
                w16 = sb.tile([P, T], BF16, name="vwin16_%d" % r, align_bytes=64)
                for piece in range(4):
                    nc.scalar.activation(out=w16[:, piece * I : (piece + 1) * I], in_=vwin[r][:, piece * I : (piece + 1) * I], func=ACT.Copy)
                nc.scalar.activation(out=g[:], in_=w16[:].indirect(offsets[:]), func=ACT.Copy)
            words = g[:].bitcast(F32)
            t = ps.tile([P, 2, P], F32, name="vT%d" % r, tag="bank_b%d" % (r % 2))
            for half in range(2):
                nc.tensor.transpose(t[:, half, :], words[:, half : I // 2 : 2], ident[:])
            vb[r] = vpair[r // 2][:, (r % 2) * I : (r % 2 + 1) * I]
            nc.scalar.copy(out=vb[r].bitcast(F32).rearrange("p (c i u) -> p c u i", u=2, i=2), in_=t[:].rearrange("p u (c i) -> p c u i", i=2))

        def quant_v(r):
            vc[r] = sb.tile([P, P], U32, name="vc%d" % r, align_bytes=64)
            vs[r] = sb.tile([P, P], U8, name="vs%d" % r, align_bytes=64)
            nc.vector.quantize_mx(out=vc[r][:].bitcast(FP8X4), scales=vs[r][:], in_=vb[r][:])

        def weights(h):
            wb[h] = sb.tile([P, P, PACK], BF16, name="wb%d" % h, tag=SHARE.get("wb%d" % h, "wb%d" % h), align_bytes=64)
            nc.vector.tensor_tensor(out=wb[h][:].rearrange("p (c i) j -> p c j i", i=2), in0=wT[h][:].rearrange("p j (c i) -> p c j i", i=2), in1=os4[:].unsqueeze(3).to_broadcast([P, P // 2, PACK, 2]), op=ALU.mult)

        def quant_w(h):
            wc[h] = sb.tile([P, P], U32, name="wc%d" % h, align_bytes=64)
            ws[h] = sb.tile([P, P], U8, name="ws%d" % h, align_bytes=64)
            nc.vector.quantize_mx(out=wc[h][:].bitcast(FP8X4), scales=ws[h][:], in_=wb[h][:].rearrange("p q j -> p (q j)"))

        ob = {}

        def product(r, h):
            if h not in ob:
                ob[h] = ps.tile([P, PACK, P], F32, name="o%d" % h, tag="bank_a%d" % h)
            nc.tensor.matmul_mx(out=ob[h][:, r, :], lhsT=vc[r].bitcast(FP8X4), lhsT_scale=vs[r],
                                rhs=wc[h][:].bitcast(FP8X4), rhs_scale=ws[h][:], start=True, stop=True)

        weave("b", 0, 1, False)
        weave("b", 1, 2, False)
        quant_q("b", 0, 1)
        weave("a", 0, 1, True)
        quant_q("a", 0, 1)
        score("b", 0)
        score("a", 0)
        weave("a", 1, 2, False)
        quant_pair()
        score("b", 1)
        score("a", 1)
        copy_b(0)
        copy_b(1)
        make_s(0)
        weave("ta", 0, 2, True)
        make_s(1)
        make_max(0)
        quant_q("ta", 0, 2)
        make_max(1)
        score("ta", 0)
        score("ta", 1)
        weave("tb", 0, 2, False)
        quant_q("tb", 0, 2)
        score("tb", 0)
        score("tb", 1)
        make_p(0)
        copy_a(0)
        make_p(1)
        copy_a(1)
        make_u(0)
        make_v(0)
        make_u(1)
        make_rz(0)
        make_v(1)
        make_ts(0, nc.vector)
        make_rz(1)
        make_tp(0)
        gather_v(0, False)
        gather_v(1, True)
        make_ts(1, nc.vector)
        gather_v(2, True)
        make_tp(1)
        gather_v(3, True)
        weights(0)
        quant_v2(0, 1)
        quant_w(0)
        quant_v2(2, 3)
        weights(1)
        quant_w(1)
        out_rows = out_0.rearrange("(p r) q -> p r q", r=PACK)
        words_out = out_1[0].rearrange("p c r -> p (c r)").bitcast(I32)
        oc = sb.tile([P, Q], U32, name="oc", align_bytes=64)
        osc = sb.tile([P, Q], U8, name="osc", align_bytes=64)
        o16 = [sb.tile([P, P, PACK], BF16, name="o16_%d" % h, align_bytes=64) for h in range(QT)]
        o32 = [sb.tile([P, PACK, P], F32, name="o32_%d" % h) for h in range(QT)]
        for r in range(PACK):
            product(r, 0)
        nc.scalar.copy(out=o32[0][:], in_=ob[0][:])
        nc.sync.dma_start(out=out_rows[:, :, 0:P], in_=o32[0][:])
        nc.scalar.copy(out=o16[0][:].rearrange("p (c i) r -> p c r i", i=2), in_=ob[0][:].rearrange("p r (c i) -> p c r i", i=2))
        nc.vector.quantize_mx(out=oc[:, 0:P].bitcast(FP8X4), scales=osc[:, 0:P], in_=o16[0][:].rearrange("p q r -> p (q r)"))
        nc.sync.dma_start(out=words_out[:, 0:P], in_=oc[:, 0:P].bitcast(I32))
        halves = [ps.tile([P, 2, P], F32, name="o1_%d" % n, tag=tag) for n, tag in enumerate(("bank_a1", "bank_tb1"))]
        for r in range(PACK):
            nc.tensor.matmul_mx(out=halves[r // 2][:, r % 2, :], lhsT=vc[r].bitcast(FP8X4), lhsT_scale=vs[r],
                                rhs=wc[1][:].bitcast(FP8X4), rhs_scale=ws[1][:], start=True, stop=True)
        nc.scalar.copy(out=o32[1][:, 0:2, :], in_=halves[0][:])
        nc.vector.tensor_copy(out=o32[1][:, 2:4, :], in_=halves[1][:])
        nc.sync.dma_start(out=out_rows[:, :, P:Q], in_=o32[1][:])
        nc.vector.tensor_copy(out=o16[1][:].rearrange("p (c i) r -> p c r i", i=4), in_=o32[1][:].rearrange("p r (c i) -> p c r i", i=4))
        nc.vector.quantize_mx(out=oc[:, P:Q].bitcast(FP8X4), scales=osc[:, P:Q], in_=o16[1][:].rearrange("p q r -> p (q r)"))
        nc.sync.dma_start(out=words_out[:, P:Q], in_=oc[:, P:Q].bitcast(I32))
        for g in range(4):
            eng = nc.scalar if g % 2 == 0 else nc.sync
            eng.dma_start(out=out_2[0, 4 * g : 4 * g + 4, :].bitcast(I32), in_=osc[32 * g : 32 * g + 4, :].bitcast(I32))
